import numpy as np
import ml_dtypes


def mxq(x, axis, fmt="e4m3"):
    dtype, down = {"e4m3": (ml_dtypes.float8_e4m3fn, 7), "e5m2": (ml_dtypes.float8_e5m2, 14)}[fmt]
    v = np.moveaxis(np.asarray(x, np.float32).astype(ml_dtypes.bfloat16).astype(np.float64), axis, -1)
    blocks = v.reshape(v.shape[:-1] + (-1, 32))
    amax = np.abs(blocks).max(-1, keepdims=True)
    byte = np.maximum(np.where(amax > 0, np.frexp(amax)[1] - 1 + 127, 0) - down, 1)
    scale = np.exp2(byte - 127.0)
    codes = (blocks / scale).astype(np.float32).astype(dtype).astype(np.float64)
    return np.moveaxis((codes * scale).reshape(v.shape), -1, axis)


WIDE = False


def mx_kscale(k, group=512):
    if not WIDE:
        return np.ones(k)
    levels = np.array([18, -18])
    if group != 512:
        return np.exp2(np.random.permutation(np.resize(levels, k // group))).repeat(group)
    if k % 512:
        return np.exp2(np.random.permutation(np.resize(levels, k // 32))).repeat(32)
    a = np.empty((k // 512, 16))
    for p in range(k // 512):
        a[p, :8] = np.random.permutation(np.resize(levels, 8))
        for g in range(8):
            far = levels[np.abs(levels - a[p, g]) >= 10]
            a[p, g + 8] = far[np.random.randint(len(far))]
    return np.exp2(a.ravel()).repeat(32)


def f64(x):
    return np.asarray(x).astype(np.float64)


K, R, M, N = 1024, 128, 512, 512


def setup_inputs():
    n = np.random.standard_normal
    s = mx_kscale(K)[:, None]
    z = mx_kscale(R, 0)
    return {
        "x": (n((K, N)) * s).astype(np.float32),
        "w": (n((K, M)) / np.sqrt(K) / s).astype(np.float32),
        "a": (n((K, R)) / np.sqrt(K) / s * z).astype(np.float32),
        "bb": (n((R, M)) / np.sqrt(R) / z[:, None]).astype(np.float32),
        "b": (0.5 * n((M, 1))).astype(np.float32),
    }


def reference(x, w, a, bb, b):
    xq = mxq(f64(x), 0, "e4m3")
    z = mxq(f64(a), 0, "e4m3").T @ xq
    y = (mxq(f64(w), 0, "e4m3").T @ xq) + (mxq(f64(bb), 0, "e4m3").T @ mxq(z, 0, "e4m3"))
    y = y + f64(b)
    y = np.maximum(y, 0.0)
    return y

@@ -1,0 +1,258 @@
+from contextlib import ExitStack
+
+import concourse.mybir as mybir
+
+K, R, M, N = 1024, 128, 512, 512
+FLOPS = 2 * K * R * N + 2 * K * M * N + 2 * R * M * N
+
+F32 = mybir.dt.float32
+BF16 = mybir.dt.bfloat16
+U32 = mybir.dt.uint32
+I32 = mybir.dt.int32
+U8 = mybir.dt.uint8
+FP8X4 = mybir.dt.float8_e4m3fn_x4
+ACT = mybir.ActivationFunctionType
+ALU = mybir.AluOpType
+
+P = 128
+PACK = 4
+K_PASS = P * PACK
+QUAD = 32
+T = 128
+
+
+def tile_rows_lora_relu_bias_kernel(tc, x, w, a, bb, b, out):
+    nc = tc.nc
+    with ExitStack() as ctx:
+        sb = ctx.enter_context(tc.tile_pool(name="sb", bufs=1))
+        ps = ctx.enter_context(tc.psum_pool(name="ps", bufs=1))
+        ctx.enter_context(tc.manual_schedule())
+
+        whole = [ps.tile([P, 512], F32, name="whole%d" % i) for i in range(4)]
+        rowb = [ps.tile([P, 512], F32, name="rowb%d" % i) for i in range(4)]
+
+        def operand(name, width):
+            return {
+                "raw": sb.tile([P, PACK, width], F32, name=name + "_raw", align_bytes=64),
+                "grp": sb.tile([P, width, PACK], BF16, name=name + "_grp", align_bytes=64),
+                "codes": sb.tile([P, width], U32, name=name + "_codes", align_bytes=64),
+                "scales": sb.tile([P, width], U8, name=name + "_scales", align_bytes=64),
+            }
+
+        def load(op, src, s, c0, width):
+            rows = src[s * K_PASS : (s + 1) * K_PASS, c0 : c0 + width]
+            nc.sync.dma_start(out=op["raw"][:], in_=rows.rearrange("(p j) c -> p j c", j=PACK))
+
+        def interleave(engine, op, c0, c1):
+            dst = op["grp"][:, c0:c1, :].rearrange("p (c i) j -> p c j i", i=4)
+            src = op["raw"][:, :, c0:c1].rearrange("p j (c i) -> p c j i", i=4)
+            if engine == "vector":
+                nc.vector.tensor_copy(out=dst, in_=src)
+            else:
+                nc.scalar.copy(out=dst, in_=src)
+
+        def quantize(op, c0, c1):
+            nc.vector.quantize_mx(
+                out=op["codes"][:, c0:c1].bitcast(FP8X4),
+                scales=op["scales"][:, c0:c1],
+                in_=op["grp"][:, c0:c1, :].rearrange("p c j -> p (c j)"),
+            )
+
+        def mx(dst, lc, ls, rc, rs, start, stop):
+            nc.tensor.matmul_mx(
+                out=dst, lhsT=lc.bitcast(FP8X4), lhsT_scale=ls, rhs=rc.bitcast(FP8X4), rhs_scale=rs,
+                start=start, stop=stop,
+            )
+
+        a_raw = sb.tile([P, 2, PACK, R], F32, align_bytes=64)
+        a_grp = sb.tile([P, 2, R * PACK], BF16, align_bytes=64)
+        a_codes1 = sb.tile([P, 2 * R], U32, align_bytes=64)
+        a_scales1 = sb.tile([P, 2 * R], U8, align_bytes=64)
+        a_codes = sb.tile([P, 8, T], U32, align_bytes=64)
+        a_scales = sb.tile([P, 8, T], U8, align_bytes=64)
+        ops = {"bb": operand("bb", T)}
+        ops["x00"] = operand("x00", 256)
+        ops["x01"] = operand("x01", 256)
+        ops["x10"] = operand("x10", 256)
+        ops["x12"] = operand("x12", 128)
+        ops["x13"] = operand("x13", 128)
+        ops["w00"] = operand("w00", 256)
+        ops["w10"] = operand("w10", 256)
+        ops["w01"] = operand("w01", 256)
+        ops["w12"] = operand("w12", 128)
+        ops["w13"] = operand("w13", 128)
+        xm = {(0, 0): ("x00", 0), (0, 1): ("x00", 128), (1, 0): ("x01", 0), (1, 1): ("x01", 128), (0, 2): ("x10", 0), (0, 3): ("x10", 128), (1, 2): ("x12", 0), (1, 3): ("x13", 0)}
+        wm = {(0, 0): ("w00", 0), (0, 1): ("w00", 128), (1, 0): ("w10", 0), (1, 1): ("w10", 128), (0, 2): ("w01", 0), (0, 3): ("w01", 128), (1, 2): ("w12", 0), (1, 3): ("w13", 0)}
+        bo = ops["bb"]
+        z_grp = sb.tile([P, N, PACK], BF16, align_bytes=64)
+        z_codes = sb.tile([P, N], U32, align_bytes=64)
+        z_scales = sb.tile([P, N], U8, align_bytes=64)
+        ops["z"] = {"grp": z_grp, "codes": z_codes, "scales": z_scales}
+        bias = sb.tile([P, 4, 8], F32)
+        low = [sb.tile([P, N], F32, name="low%d" % g) for g in range(4)]
+        tot = [sb.tile([P, N], F32, name="tot%d" % g) for g in range(4)]
+        res = [sb.tile([P, N], F32, name="res%d" % g) for g in range(4)]
+
+        with nc.allow_non_contiguous_dma(reason="one bias a partition"):
+            nc.scalar.dma_start(out=bias[:, :, 0:1], in_=b.rearrange("(g p) o -> p g o", p=P))
+        nc.sync.dma_start(out=a_raw[:].rearrange("p s j r -> p s (j r)"), in_=a.rearrange("(s p j) r -> p s (j r)", s=2, j=PACK))
+        load(ops["x00"], x, 0, 0, 256)
+        load(ops["x01"], x, 1, 0, 256)
+        load(ops["x10"], x, 0, 256, 256)
+        load(ops["x12"], x, 1, 256, 128)
+        load(ops["x13"], x, 1, 384, 128)
+        for g in (0, 2, 1, 3):
+            nc.sync.dma_start(out=bo["raw"][QUAD * g : QUAD * (g + 1), :, :], in_=bb[:, T * g : T * (g + 1)].rearrange("(p j) c -> p j c", j=PACK))
+        load(ops["w00"], w, 0, 0, 256)
+        load(ops["w10"], w, 1, 0, 256)
+        load(ops["w01"], w, 0, 256, 256)
+        load(ops["w12"], w, 1, 256, 128)
+        load(ops["w13"], w, 1, 384, 128)
+
+        nc.vector.memset(a_scales1[:].bitcast(U32), 0)
+
+        def deal_a(engine, s):
+            dst = a_grp[:, s, :].rearrange("p (t m j) -> p m j t", t=4, j=PACK)
+            src = a_raw[:, s, :, :].rearrange("p j (m t) -> p m j t", t=4)
+            if engine == "vector":
+                nc.vector.tensor_copy(out=dst, in_=src)
+            else:
+                nc.scalar.activation(out=dst, in_=src, func=ACT.Copy)
+
+        def quantize_a():
+            nc.vector.quantize_mx(
+                out=a_codes1[:].bitcast(FP8X4), scales=a_scales1[:], in_=a_grp[:].rearrange("p s c -> p (s c)")
+            )
+
+        def replicate_a():
+            nc.vector.tensor_copy(
+                out=a_codes[:].bitcast(I32).rearrange("p u (g m) -> p u g m", g=4),
+                in_=a_codes1[:].bitcast(I32).rearrange("p (u m) -> p u m", m=QUAD).unsqueeze(2).to_broadcast([P, 8, 4, QUAD]),
+            )
+            nc.vector.tensor_copy(
+                out=a_scales[:].bitcast(I32).rearrange("p u (g m) -> p u g m", g=4),
+                in_=a_scales1[:].bitcast(I32).rearrange("p (u m) -> p u m", m=8).unsqueeze(2).to_broadcast([P, 8, 4, 8]),
+            )
+
+        def window(table, s, i):
+            name, c0 = table[s, i]
+            return ops[name]["codes"][:, c0 : c0 + T], ops[name]["scales"][:, c0 : c0 + T]
+
+        def z_chunk(c, bank):
+            for t in range(4):
+                for s in range(2):
+                    xc, xs = window(xm, s, c)
+                    mx(whole[bank][:, T * t : T * (t + 1)], a_codes[:, 4 * s + t, :], a_scales[:, 4 * s + t, :],
+                       xc, xs, s == 0, s == 1)
+
+        def copy(engine, dst, src):
+            if engine == "vector":
+                nc.vector.tensor_copy(out=dst, in_=src)
+            else:
+                nc.scalar.copy(out=dst, in_=src)
+
+        def z_out(engine, c, bank):
+            copy(engine, z_grp[:, T * c : T * (c + 1), :], whole[bank][:].rearrange("p (t n) -> p n t", t=4))
+
+        def low_rank(c):
+            cols = slice(T * c, T * (c + 1))
+            for g in range(4):
+                rows = slice(QUAD * g, QUAD * (g + 1))
+                mx(rowb[g][:, cols], bo["codes"][rows, :], bo["scales"][rows, :],
+                   z_codes[rows, cols], z_scales[rows, cols], True, True)
+
+        def low_out(engine, g, c0, c1):
+            copy(engine, low[g][:, T * c0 : T * c1], rowb[g][:, T * c0 : T * c1])
+
+        def y_part(bank, g, c0, c1):
+            for c in range(c0, c1):
+                for s in range(2):
+                    wc, ws = window(wm, s, g)
+                    xc, xs = window(xm, s, c)
+                    mx(whole[bank][:, T * c : T * (c + 1)], wc, ws, xc, xs, s == 0, s == 1)
+
+        def add(bank, g, c0, c1):
+            cols = slice(T * c0, T * c1)
+            nc.vector.tensor_tensor(out=tot[g][:, cols], in0=whole[bank][:, cols], in1=low[g][:, cols], op=ALU.add)
+
+        def finish(engine, g, c0, c1, queue):
+            cols = slice(T * c0, T * c1)
+            if engine == "vector":
+                nc.vector.tensor_scalar(out=res[g][:, cols], in0=tot[g][:, cols], scalar1=bias[:, g, 0:1], scalar2=0.0, op0=ALU.add, op1=ALU.max)
+            elif engine == "gpsimd":
+                nc.gpsimd.tensor_scalar(out=res[g][:, cols], in0=tot[g][:, cols], scalar1=bias[:, g, 0:1], scalar2=0.0, op0=ALU.add, op1=ALU.max)
+            else:
+                nc.scalar.activation(out=res[g][:, cols], in_=tot[g][:, cols], func=ACT.Relu, bias=bias[:, g, 0:1])
+            if queue == "sync":
+                nc.sync.dma_start(out=out[T * g : T * (g + 1), cols], in_=res[g][:, cols])
+            else:
+                nc.scalar.dma_start(out=out[T * g : T * (g + 1), cols], in_=res[g][:, cols])
+
+        deal_a("vector", 0)
+        deal_a("scalar", 1)
+        quantize_a()
+        interleave("scalar", ops["x00"], 0, 256)
+        replicate_a()
+        interleave("scalar", ops["x01"], 128, 256)
+        interleave("vector", ops["x01"], 0, 128)
+        quantize(ops["x01"], 0, 256)
+        quantize(ops["x00"], 0, 256)
+        interleave("scalar", ops["x10"], 128, 256)
+        interleave("vector", ops["x10"], 0, 128)
+        interleave("vector", ops["x12"], 0, 128)
+        interleave("scalar", ops["x13"], 0, 128)
+        z_chunk(0, 0)
+        quantize(ops["x10"], 0, 256)
+        z_chunk(1, 1)
+        quantize(ops["x13"], 0, 128)
+        interleave("vector", ops["bb"], 0, 128)
+        z_out("scalar", 0, 0)
+        interleave("scalar", ops["w00"], 32, 256)
+        quantize(ops["x12"], 0, 128)
+        z_chunk(3, 3)
+        z_chunk(2, 2)
+        z_out("vector", 1, 1)
+        quantize(ops["bb"], 0, 128)
+        z_out("scalar", 3, 3)
+        quantize(ops["z"], 0, 256)
+        interleave("vector", ops["w00"], 0, 32)
+        interleave("vector", ops["w10"], 0, 256)
+        quantize(ops["z"], 384, 512)
+        low_rank(3)
+        low_rank(1)
+        quantize(ops["w10"], 0, 256)
+        z_out("scalar", 2, 2)
+        interleave("scalar", ops["w01"], 0, 256)
+        quantize(ops["z"], 256, 384)
+        quantize(ops["w00"], 0, 256)
+        low_rank(0)
+        low_rank(2)
+        y_part(0, 0, 0, 4)
+        interleave("vector", ops["w12"], 0, 128)
+        interleave("scalar", ops["w13"], 96, 128)
+        low_out("vector", 1, 2, 4)
+        quantize(ops["w12"], 0, 128)
+        interleave("vector", ops["w13"], 0, 96)
+        quantize(ops["w01"], 0, 256)
+        low_out("scalar", 0, 2, 4)
+        low_out("scalar", 0, 0, 2)
+        y_part(1, 1, 0, 4)
+        quantize(ops["w13"], 0, 128)
+        add(0, 0, 0, 4)
+        low_out("scalar", 1, 0, 2)
+        low_out("scalar", 3, 0, 2)
+        low_out("scalar", 3, 2, 4)
+        add(1, 1, 0, 4)
+        finish("vector", 0, 0, 4, "sync")
+        y_part(2, 2, 0, 4)
+        low_out("scalar", 2, 0, 2)
+        low_out("scalar", 2, 2, 4)
+        y_part(3, 3, 0, 2)
+        y_part(0, 3, 2, 4)
+        add(2, 2, 0, 4)
+        add(3, 3, 0, 2)
+        finish("scalar", 1, 0, 4, "sync")
+        finish("vector", 2, 0, 4, "sync")
+        finish("scalar", 3, 0, 2, "sync")
+        add(0, 3, 2, 4)
+        finish("vector", 3, 2, 4, "sync")

@@ -71,8 +71,8 @@ def tile_rows_lora_relu_bias_kernel(tc, x, w, a, bb, b, out):
         a_codes = sb.tile([P, 8, T], U32, align_bytes=64)
         a_scales = sb.tile([P, 8, T], U8, align_bytes=64)
         ops = {"bb": operand("bb", T)}
-        ops["x00"] = operand("x00", 256)
         ops["x01"] = operand("x01", 256)
+        ops["x00"] = operand("x00", 256)
         ops["x10"] = operand("x10", 256)
         ops["x12"] = operand("x12", 128)
         ops["x13"] = operand("x13", 128)
@@ -88,16 +88,19 @@ def tile_rows_lora_relu_bias_kernel(tc, x, w, a, bb, b, out):
         z_codes = sb.tile([P, N], U32, align_bytes=64)
         z_scales = sb.tile([P, N], U8, align_bytes=64)
         ops["z"] = {"grp": z_grp, "codes": z_codes, "scales": z_scales}
-        bias = sb.tile([P, 4, 8], F32)
+        bias_rows = sb.tile([P, QUAD], F32, align_bytes=64)
+        bias = sb.tile([P, QUAD], F32, align_bytes=64)
         low = [sb.tile([P, N], F32, name="low%d" % g) for g in range(4)]
         tot = [sb.tile([P, N], F32, name="tot%d" % g) for g in range(4)]
         res = [sb.tile([P, N], F32, name="res%d" % g) for g in range(4)]
 
-        with nc.allow_non_contiguous_dma(reason="one bias a partition"):
-            nc.scalar.dma_start(out=bias[:, :, 0:1], in_=b.rearrange("(g p) o -> p g o", p=P))
+        nc.vector.memset(bias_rows[:], 0.0)
+        b_rows = b.rearrange("(g q i) o -> q g (i o)", g=4, q=4)
+        for q in range(4):
+            nc.scalar.dma_start(out=bias_rows[QUAD * q : QUAD * q + 4, :], in_=b_rows[q])
         nc.sync.dma_start(out=a_raw[:].rearrange("p s j r -> p s (j r)"), in_=a.rearrange("(s p j) r -> p s (j r)", s=2, j=PACK))
-        load(ops["x00"], x, 0, 0, 256)
         load(ops["x01"], x, 1, 0, 256)
+        load(ops["x00"], x, 0, 0, 256)
         load(ops["x10"], x, 0, 256, 256)
         load(ops["x12"], x, 1, 256, 128)
         load(ops["x13"], x, 1, 384, 128)
@@ -112,11 +115,13 @@ def tile_rows_lora_relu_bias_kernel(tc, x, w, a, bb, b, out):
         nc.vector.memset(a_scales1[:].bitcast(U32), 0)
 
         def deal_a(engine, s):
-            dst = a_grp[:, s, :].rearrange("p (t m j) -> p m j t", t=4, j=PACK)
-            src = a_raw[:, s, :, :].rearrange("p j (m t) -> p m j t", t=4)
             if engine == "vector":
+                dst = a_grp[:, s, :].rearrange("p (t m j) -> p t m j", t=4, j=PACK)
+                src = a_raw[:, s, :, :].rearrange("p j (m t) -> p t m j", t=4)
                 nc.vector.tensor_copy(out=dst, in_=src)
             else:
+                dst = a_grp[:, s, :].rearrange("p (t m j) -> p m t j", t=4, j=PACK)
+                src = a_raw[:, s, :, :].rearrange("p j (m t) -> p m t j", t=4)
                 nc.scalar.activation(out=dst, in_=src, func=ACT.Copy)
 
         def quantize_a():
@@ -178,11 +183,11 @@ def tile_rows_lora_relu_bias_kernel(tc, x, w, a, bb, b, out):
         def finish(engine, g, c0, c1, queue):
             cols = slice(T * c0, T * c1)
             if engine == "vector":
-                nc.vector.tensor_scalar(out=res[g][:, cols], in0=tot[g][:, cols], scalar1=bias[:, g, 0:1], scalar2=0.0, op0=ALU.add, op1=ALU.max)
+                nc.vector.tensor_scalar(out=res[g][:, cols], in0=tot[g][:, cols], scalar1=bias[:, g : g + 1], scalar2=0.0, op0=ALU.add, op1=ALU.max)
             elif engine == "gpsimd":
-                nc.gpsimd.tensor_scalar(out=res[g][:, cols], in0=tot[g][:, cols], scalar1=bias[:, g, 0:1], scalar2=0.0, op0=ALU.add, op1=ALU.max)
+                nc.gpsimd.tensor_scalar(out=res[g][:, cols], in0=tot[g][:, cols], scalar1=bias[:, g : g + 1], scalar2=0.0, op0=ALU.add, op1=ALU.max)
             else:
-                nc.scalar.activation(out=res[g][:, cols], in_=tot[g][:, cols], func=ACT.Relu, bias=bias[:, g, 0:1])
+                nc.scalar.activation(out=res[g][:, cols], in_=tot[g][:, cols], func=ACT.Relu, bias=bias[:, g : g + 1])
             if queue == "sync":
                 nc.sync.dma_start(out=out[T * g : T * (g + 1), cols], in_=res[g][:, cols])
             else:
@@ -190,69 +195,77 @@ def tile_rows_lora_relu_bias_kernel(tc, x, w, a, bb, b, out):
 
         deal_a("vector", 0)
         deal_a("scalar", 1)
+        nc.vector.transpose(out=bias[:], in_=bias_rows[:])
         quantize_a()
-        interleave("scalar", ops["x00"], 0, 256)
+        interleave("vector", ops["x01"], 0, 256)
         replicate_a()
-        interleave("scalar", ops["x01"], 128, 256)
-        interleave("vector", ops["x01"], 0, 128)
+        interleave("scalar", ops["x00"], 0, 256)
+        interleave("scalar", ops["x12"], 0, 128)
         quantize(ops["x01"], 0, 256)
-        quantize(ops["x00"], 0, 256)
-        interleave("scalar", ops["x10"], 128, 256)
-        interleave("vector", ops["x10"], 0, 128)
-        interleave("vector", ops["x12"], 0, 128)
         interleave("scalar", ops["x13"], 0, 128)
-        z_chunk(0, 0)
-        quantize(ops["x10"], 0, 256)
+        interleave("scalar", ops["bb"], 0, 128)
+        quantize(ops["x00"], 0, 256)
         z_chunk(1, 1)
+        interleave("vector", ops["x10"], 0, 256)
+        quantize(ops["x10"], 0, 256)
+        z_chunk(0, 0)
         quantize(ops["x13"], 0, 128)
-        interleave("vector", ops["bb"], 0, 128)
-        z_out("scalar", 0, 0)
-        interleave("scalar", ops["w00"], 32, 256)
+        z_out("vector", 1, 1)
         quantize(ops["x12"], 0, 128)
+        z_out("scalar", 0, 0)
+        quantize(ops["bb"], 0, 128)
         z_chunk(3, 3)
         z_chunk(2, 2)
-        z_out("vector", 1, 1)
-        quantize(ops["bb"], 0, 128)
-        z_out("scalar", 3, 3)
+        interleave("vector", ops["w00"], 0, 192)
         quantize(ops["z"], 0, 256)
-        interleave("vector", ops["w00"], 0, 32)
-        interleave("vector", ops["w10"], 0, 256)
-        quantize(ops["z"], 384, 512)
-        low_rank(3)
-        low_rank(1)
-        quantize(ops["w10"], 0, 256)
-        z_out("scalar", 2, 2)
-        interleave("scalar", ops["w01"], 0, 256)
-        quantize(ops["z"], 256, 384)
+        interleave("scalar", ops["w00"], 192, 256)
         quantize(ops["w00"], 0, 256)
         low_rank(0)
-        low_rank(2)
-        y_part(0, 0, 0, 4)
-        interleave("vector", ops["w12"], 0, 128)
-        interleave("scalar", ops["w13"], 96, 128)
-        low_out("vector", 1, 2, 4)
-        quantize(ops["w12"], 0, 128)
-        interleave("vector", ops["w13"], 0, 96)
-        quantize(ops["w01"], 0, 256)
-        low_out("scalar", 0, 2, 4)
+        z_out("scalar", 3, 3)
+        quantize(ops["z"], 384, 512)
+        z_out("scalar", 2, 2)
+        low_rank(1)
+        interleave("vector", ops["w10"], 0, 256)
         low_out("scalar", 0, 0, 2)
-        y_part(1, 1, 0, 4)
-        quantize(ops["w13"], 0, 128)
-        add(0, 0, 0, 4)
-        low_out("scalar", 1, 0, 2)
-        low_out("scalar", 3, 0, 2)
-        low_out("scalar", 3, 2, 4)
-        add(1, 1, 0, 4)
-        finish("vector", 0, 0, 4, "sync")
-        y_part(2, 2, 0, 4)
-        low_out("scalar", 2, 0, 2)
+        low_rank(3)
+        quantize(ops["z"], 256, 384)
+        quantize(ops["w10"], 0, 256)
+        interleave("vector", ops["w01"], 0, 160)
+        interleave("vector", ops["w12"], 0, 128)
+        interleave("scalar", ops["w01"], 160, 256)
+        low_rank(2)
+        low_out("scalar", 1, 2, 4)
+        y_part(2, 0, 2, 4)
+        y_part(2, 0, 0, 2)
+        y_part(1, 1, 0, 2)
         low_out("scalar", 2, 2, 4)
-        y_part(3, 3, 0, 2)
-        y_part(0, 3, 2, 4)
-        add(2, 2, 0, 4)
-        add(3, 3, 0, 2)
-        finish("scalar", 1, 0, 4, "sync")
-        finish("vector", 2, 0, 4, "sync")
-        finish("scalar", 3, 0, 2, "sync")
-        add(0, 3, 2, 4)
+        quantize(ops["w01"], 0, 256)
+        quantize(ops["w12"], 0, 128)
+        low_out("scalar", 0, 2, 4)
+        low_out("vector", 1, 0, 2)
+        low_out("scalar", 3, 2, 4)
+        add(2, 0, 2, 4)
+        y_part(0, 1, 2, 4)
+        y_part(3, 2, 2, 4)
+        interleave("scalar", ops["w13"], 0, 128)
+        low_out("scalar", 2, 0, 2)
+        add(1, 1, 0, 2)
+        add(2, 0, 0, 2)
+        quantize(ops["w13"], 0, 128)
+        finish("scalar", 1, 0, 2, "sync")
+        y_part(0, 2, 0, 2)
+        low_out("scalar", 3, 0, 2)
+        finish("vector", 0, 2, 4, "sync")
+        add(3, 2, 2, 4)
+        finish("scalar", 0, 0, 2, "sync")
+        add(0, 1, 2, 4)
+        y_part(1, 3, 2, 4)
+        finish("scalar", 2, 2, 4, "sync")
+        add(0, 2, 0, 2)
+        y_part(2, 3, 0, 2)
+        finish("scalar", 1, 2, 4, "sync")
+        finish("scalar", 2, 0, 2, "sync")
+        add(1, 3, 2, 4)
+        add(2, 3, 0, 2)
         finish("vector", 3, 2, 4, "sync")
+        finish("vector", 3, 0, 2, "sync")

@@ -74,13 +74,13 @@ def tile_rows_lora_relu_bias_kernel(tc, x, w, a, bb, b, out):
         ops["x01"] = operand("x01", 256)
         ops["x00"] = operand("x00", 256)
         ops["x10"] = operand("x10", 256)
-        ops["x12"] = operand("x12", 128)
         ops["x13"] = operand("x13", 128)
-        ops["w00"] = operand("w00", 256)
+        ops["x12"] = operand("x12", 128)
         ops["w10"] = operand("w10", 256)
+        ops["w00"] = operand("w00", 256)
         ops["w01"] = operand("w01", 256)
-        ops["w12"] = operand("w12", 128)
         ops["w13"] = operand("w13", 128)
+        ops["w12"] = operand("w12", 128)
         xm = {(0, 0): ("x00", 0), (0, 1): ("x00", 128), (1, 0): ("x01", 0), (1, 1): ("x01", 128), (0, 2): ("x10", 0), (0, 3): ("x10", 128), (1, 2): ("x12", 0), (1, 3): ("x13", 0)}
         wm = {(0, 0): ("w00", 0), (0, 1): ("w00", 128), (1, 0): ("w10", 0), (1, 1): ("w10", 128), (0, 2): ("w01", 0), (0, 3): ("w01", 128), (1, 2): ("w12", 0), (1, 3): ("w13", 0)}
         bo = ops["bb"]
@@ -101,16 +101,16 @@ def tile_rows_lora_relu_bias_kernel(tc, x, w, a, bb, b, out):
         nc.sync.dma_start(out=a_raw[:].rearrange("p s j r -> p s (j r)"), in_=a.rearrange("(s p j) r -> p s (j r)", s=2, j=PACK))
         load(ops["x01"], x, 1, 0, 256)
         load(ops["x00"], x, 0, 0, 256)
-        load(ops["x10"], x, 0, 256, 256)
-        load(ops["x12"], x, 1, 256, 128)
-        load(ops["x13"], x, 1, 384, 128)
         for g in (0, 2, 1, 3):
             nc.sync.dma_start(out=bo["raw"][QUAD * g : QUAD * (g + 1), :, :], in_=bb[:, T * g : T * (g + 1)].rearrange("(p j) c -> p j c", j=PACK))
-        load(ops["w00"], w, 0, 0, 256)
+        load(ops["x10"], x, 0, 256, 256)
+        load(ops["x13"], x, 1, 384, 128)
+        load(ops["x12"], x, 1, 256, 128)
         load(ops["w10"], w, 1, 0, 256)
+        load(ops["w00"], w, 0, 0, 256)
         load(ops["w01"], w, 0, 256, 256)
-        load(ops["w12"], w, 1, 256, 128)
         load(ops["w13"], w, 1, 384, 128)
+        load(ops["w12"], w, 1, 256, 128)
 
         nc.vector.memset(a_scales1[:].bitcast(U32), 0)
 
@@ -138,6 +138,11 @@ def tile_rows_lora_relu_bias_kernel(tc, x, w, a, bb, b, out):
                 out=a_scales[:].bitcast(I32).rearrange("p u (g m) -> p u g m", g=4),
                 in_=a_scales1[:].bitcast(I32).rearrange("p (u m) -> p u m", m=8).unsqueeze(2).to_broadcast([P, 8, 4, 8]),
             )
+
+        def warm(bank, count):
+            for i in range(count):
+                cols = slice(T * (i % 4), T * (i % 4 + 1))
+                mx(whole[bank][:, cols], a_codes1[:, 0:T], a_scales1[:, 0:T], a_codes1[:, T : 2 * T], a_scales1[:, T : 2 * T], True, True)
 
         def window(table, s, i):
             name, c0 = table[s, i]
@@ -193,79 +198,84 @@ def tile_rows_lora_relu_bias_kernel(tc, x, w, a, bb, b, out):
             else:
                 nc.scalar.dma_start(out=out[T * g : T * (g + 1), cols], in_=res[g][:, cols])
 
-        deal_a("vector", 0)
         deal_a("scalar", 1)
-        nc.vector.transpose(out=bias[:], in_=bias_rows[:])
+        deal_a("vector", 0)
         quantize_a()
-        interleave("vector", ops["x01"], 0, 256)
+        warm(3, 16)
         replicate_a()
-        interleave("scalar", ops["x00"], 0, 256)
-        interleave("scalar", ops["x12"], 0, 128)
-        quantize(ops["x01"], 0, 256)
-        interleave("scalar", ops["x13"], 0, 128)
+        interleave("vector", ops["x00"], 0, 256)
+        interleave("scalar", ops["x01"], 0, 256)
         interleave("scalar", ops["bb"], 0, 128)
+        quantize(ops["x01"], 0, 256)
         quantize(ops["x00"], 0, 256)
-        z_chunk(1, 1)
-        interleave("vector", ops["x10"], 0, 256)
-        quantize(ops["x10"], 0, 256)
+        nc.vector.transpose(out=bias[:], in_=bias_rows[:])
+        interleave("scalar", ops["x10"], 160, 256)
+        interleave("vector", ops["x10"], 0, 160)
         z_chunk(0, 0)
-        quantize(ops["x13"], 0, 128)
-        z_out("vector", 1, 1)
-        quantize(ops["x12"], 0, 128)
+        interleave("vector", ops["x13"], 0, 128)
         z_out("scalar", 0, 0)
-        quantize(ops["bb"], 0, 128)
-        z_chunk(3, 3)
+        z_chunk(1, 1)
+        quantize(ops["x10"], 0, 256)
+        quantize(ops["x13"], 0, 128)
+        interleave("vector", ops["x12"], 0, 128)
+        z_chunk(3, 0)
+        quantize(ops["x12"], 0, 128)
+        z_out("scalar", 1, 1)
         z_chunk(2, 2)
-        interleave("vector", ops["w00"], 0, 192)
+        interleave("scalar", ops["w10"], 160, 256)
+        interleave("vector", ops["w10"], 0, 160)
+        z_out("scalar", 3, 0)
         quantize(ops["z"], 0, 256)
         interleave("scalar", ops["w00"], 192, 256)
-        quantize(ops["w00"], 0, 256)
-        low_rank(0)
-        z_out("scalar", 3, 3)
-        quantize(ops["z"], 384, 512)
+        quantize(ops["bb"], 0, 128)
         z_out("scalar", 2, 2)
-        low_rank(1)
-        interleave("vector", ops["w10"], 0, 256)
-        low_out("scalar", 0, 0, 2)
-        low_rank(3)
-        quantize(ops["z"], 256, 384)
         quantize(ops["w10"], 0, 256)
-        interleave("vector", ops["w01"], 0, 160)
-        interleave("vector", ops["w12"], 0, 128)
-        interleave("scalar", ops["w01"], 160, 256)
-        low_rank(2)
-        low_out("scalar", 1, 2, 4)
-        y_part(2, 0, 2, 4)
+        interleave("vector", ops["w00"], 0, 192)
+        quantize(ops["z"], 384, 512)
+        low_rank(1)
+        low_rank(0)
+        warm(3, 8)
+        quantize(ops["w00"], 0, 256)
+        low_out("scalar", 1, 0, 2)
         y_part(2, 0, 0, 2)
-        y_part(1, 1, 0, 2)
-        low_out("scalar", 2, 2, 4)
-        quantize(ops["w01"], 0, 256)
-        quantize(ops["w12"], 0, 128)
-        low_out("scalar", 0, 2, 4)
-        low_out("vector", 1, 0, 2)
-        low_out("scalar", 3, 2, 4)
-        add(2, 0, 2, 4)
-        y_part(0, 1, 2, 4)
-        y_part(3, 2, 2, 4)
-        interleave("scalar", ops["w13"], 0, 128)
         low_out("scalar", 2, 0, 2)
-        add(1, 1, 0, 2)
+        interleave("vector", ops["w01"], 0, 256)
+        low_out("scalar", 0, 0, 2)
+        quantize(ops["z"], 256, 384)
+        y_part(1, 1, 0, 2)
+        interleave("vector", ops["w13"], 0, 64)
+        low_rank(3)
+        low_rank(2)
+        quantize(ops["w01"], 0, 256)
         add(2, 0, 0, 2)
+        interleave("scalar", ops["w13"], 64, 128)
         quantize(ops["w13"], 0, 128)
-        finish("scalar", 1, 0, 2, "sync")
-        y_part(0, 2, 0, 2)
+        interleave("scalar", ops["w12"], 32, 128)
+        low_out("scalar", 1, 2, 4)
+        y_part(3, 1, 2, 4)
+        interleave("vector", ops["w12"], 0, 32)
+        add(1, 1, 0, 2)
+        y_part(0, 0, 2, 4)
+        low_out("scalar", 0, 2, 4)
+        y_part(0, 3, 0, 2)
+        quantize(ops["w12"], 0, 128)
+        y_part(2, 2, 0, 2)
+        low_out("scalar", 2, 2, 4)
+        finish("vector", 0, 0, 2, "sync")
         low_out("scalar", 3, 0, 2)
-        finish("vector", 0, 2, 4, "sync")
-        add(3, 2, 2, 4)
-        finish("scalar", 0, 0, 2, "sync")
-        add(0, 1, 2, 4)
-        y_part(1, 3, 2, 4)
-        finish("scalar", 2, 2, 4, "sync")
-        add(0, 2, 0, 2)
-        y_part(2, 3, 0, 2)
+        add(3, 1, 2, 4)
+        finish("vector", 1, 0, 2, "sync")
+        add(0, 0, 2, 4)
+        y_part(1, 2, 2, 4)
+        low_out("scalar", 3, 2, 4)
+        add(0, 3, 0, 2)
+        add(2, 2, 0, 2)
+        add(1, 2, 2, 4)
+        y_part(3, 3, 2, 4)
+        add(3, 3, 2, 4)
         finish("scalar", 1, 2, 4, "sync")
+        finish("scalar", 0, 2, 4, "sync")
+        finish("scalar", 3, 0, 2, "sync")
         finish("scalar", 2, 0, 2, "sync")
-        add(1, 3, 2, 4)
-        add(2, 3, 0, 2)
+        finish("vector", 2, 2, 4, "sync")
         finish("vector", 3, 2, 4, "sync")
-        finish("vector", 3, 0, 2, "sync")

@@ -71,18 +71,13 @@ def tile_rows_lora_relu_bias_kernel(tc, x, w, a, bb, b, out):
         a_codes = sb.tile([P, 8, T], U32, align_bytes=64)
         a_scales = sb.tile([P, 8, T], U8, align_bytes=64)
         ops = {"bb": operand("bb", T)}
-        ops["x01"] = operand("x01", 256)
-        ops["x00"] = operand("x00", 256)
-        ops["x10"] = operand("x10", 256)
-        ops["x13"] = operand("x13", 128)
-        ops["x12"] = operand("x12", 128)
+        ops["x0"] = operand("x0", 512)
+        ops["x1"] = operand("x1", 512)
+        ops["w0"] = operand("w0", 512)
         ops["w10"] = operand("w10", 256)
-        ops["w00"] = operand("w00", 256)
-        ops["w01"] = operand("w01", 256)
-        ops["w13"] = operand("w13", 128)
-        ops["w12"] = operand("w12", 128)
-        xm = {(0, 0): ("x00", 0), (0, 1): ("x00", 128), (1, 0): ("x01", 0), (1, 1): ("x01", 128), (0, 2): ("x10", 0), (0, 3): ("x10", 128), (1, 2): ("x12", 0), (1, 3): ("x13", 0)}
-        wm = {(0, 0): ("w00", 0), (0, 1): ("w00", 128), (1, 0): ("w10", 0), (1, 1): ("w10", 128), (0, 2): ("w01", 0), (0, 3): ("w01", 128), (1, 2): ("w12", 0), (1, 3): ("w13", 0)}
+        ops["w11"] = operand("w11", 256)
+        xm = {(0, 0): ("x0", 0), (0, 1): ("x0", 128), (0, 2): ("x0", 256), (0, 3): ("x0", 384), (1, 0): ("x1", 0), (1, 1): ("x1", 128), (1, 2): ("x1", 256), (1, 3): ("x1", 384)}
+        wm = {(0, 0): ("w0", 0), (0, 1): ("w0", 128), (0, 2): ("w0", 256), (0, 3): ("w0", 384), (1, 0): ("w10", 0), (1, 1): ("w10", 128), (1, 2): ("w11", 0), (1, 3): ("w11", 128)}
         bo = ops["bb"]
         z_grp = sb.tile([P, N, PACK], BF16, align_bytes=64)
         z_codes = sb.tile([P, N], U32, align_bytes=64)
@@ -99,18 +94,13 @@ def tile_rows_lora_relu_bias_kernel(tc, x, w, a, bb, b, out):
         for q in range(4):
             nc.scalar.dma_start(out=bias_rows[QUAD * q : QUAD * q + 4, :], in_=b_rows[q])
         nc.sync.dma_start(out=a_raw[:].rearrange("p s j r -> p s (j r)"), in_=a.rearrange("(s p j) r -> p s (j r)", s=2, j=PACK))
-        load(ops["x01"], x, 1, 0, 256)
-        load(ops["x00"], x, 0, 0, 256)
+        load(ops["x0"], x, 0, 0, 512)
+        load(ops["x1"], x, 1, 0, 512)
         for g in (0, 2, 1, 3):
             nc.sync.dma_start(out=bo["raw"][QUAD * g : QUAD * (g + 1), :, :], in_=bb[:, T * g : T * (g + 1)].rearrange("(p j) c -> p j c", j=PACK))
-        load(ops["x10"], x, 0, 256, 256)
-        load(ops["x13"], x, 1, 384, 128)
-        load(ops["x12"], x, 1, 256, 128)
+        load(ops["w0"], w, 0, 0, 512)
         load(ops["w10"], w, 1, 0, 256)
-        load(ops["w00"], w, 0, 0, 256)
-        load(ops["w01"], w, 0, 256, 256)
-        load(ops["w13"], w, 1, 384, 128)
-        load(ops["w12"], w, 1, 256, 128)
+        load(ops["w11"], w, 1, 256, 256)
 
         nc.vector.memset(a_scales1[:].bitcast(U32), 0)
 
@@ -185,7 +175,7 @@ def tile_rows_lora_relu_bias_kernel(tc, x, w, a, bb, b, out):
             cols = slice(T * c0, T * c1)
             nc.vector.tensor_tensor(out=tot[g][:, cols], in0=whole[bank][:, cols], in1=low[g][:, cols], op=ALU.add)
 
-        def finish(engine, g, c0, c1, queue):
+        def finish(engine, g, c0, c1):
             cols = slice(T * c0, T * c1)
             if engine == "vector":
                 nc.vector.tensor_scalar(out=res[g][:, cols], in0=tot[g][:, cols], scalar1=bias[:, g : g + 1], scalar2=0.0, op0=ALU.add, op1=ALU.max)
@@ -193,89 +183,96 @@ def tile_rows_lora_relu_bias_kernel(tc, x, w, a, bb, b, out):
                 nc.gpsimd.tensor_scalar(out=res[g][:, cols], in0=tot[g][:, cols], scalar1=bias[:, g : g + 1], scalar2=0.0, op0=ALU.add, op1=ALU.max)
             else:
                 nc.scalar.activation(out=res[g][:, cols], in_=tot[g][:, cols], func=ACT.Relu, bias=bias[:, g : g + 1])
-            if queue == "sync":
-                nc.sync.dma_start(out=out[T * g : T * (g + 1), cols], in_=res[g][:, cols])
-            else:
-                nc.scalar.dma_start(out=out[T * g : T * (g + 1), cols], in_=res[g][:, cols])
+
+        def store(g, c0, c1):
+            cols = slice(T * c0, T * c1)
+            nc.sync.dma_start(out=out[T * g : T * (g + 1), cols], in_=res[g][:, cols])
 
         deal_a("scalar", 1)
         deal_a("vector", 0)
         quantize_a()
-        warm(3, 16)
         replicate_a()
-        interleave("vector", ops["x00"], 0, 256)
-        interleave("scalar", ops["x01"], 0, 256)
-        interleave("scalar", ops["bb"], 0, 128)
-        quantize(ops["x01"], 0, 256)
-        quantize(ops["x00"], 0, 256)
+        interleave("vector", ops["x0"], 0, 128)
+        interleave("scalar", ops["x0"], 256, 384)
+        interleave("vector", ops["x0"], 128, 256)
+        quantize(ops["x0"], 0, 256)
+        interleave("vector", ops["x0"], 384, 512)
         nc.vector.transpose(out=bias[:], in_=bias_rows[:])
-        interleave("scalar", ops["x10"], 160, 256)
-        interleave("vector", ops["x10"], 0, 160)
-        z_chunk(0, 0)
-        interleave("vector", ops["x13"], 0, 128)
-        z_out("scalar", 0, 0)
-        z_chunk(1, 1)
-        quantize(ops["x10"], 0, 256)
-        quantize(ops["x13"], 0, 128)
-        interleave("vector", ops["x12"], 0, 128)
-        z_chunk(3, 0)
-        quantize(ops["x12"], 0, 128)
-        z_out("scalar", 1, 1)
-        z_chunk(2, 2)
-        interleave("scalar", ops["w10"], 160, 256)
-        interleave("vector", ops["w10"], 0, 160)
-        z_out("scalar", 3, 0)
-        quantize(ops["z"], 0, 256)
-        interleave("scalar", ops["w00"], 192, 256)
+        interleave("vector", ops["x1"], 0, 128)
+        quantize(ops["x1"], 0, 128)
+        interleave("scalar", ops["x1"], 128, 256)
+        quantize(ops["x1"], 128, 256)
+        quantize(ops["x0"], 256, 512)
+        z_chunk(0, 1)
+        interleave("vector", ops["x1"], 256, 384)
+        z_chunk(1, 3)
+        interleave("scalar", ops["x1"], 384, 512)
+        z_out("scalar", 0, 1)
+        interleave("vector", ops["bb"], 0, 128)
+        quantize(ops["x1"], 384, 512)
+        quantize(ops["x1"], 256, 384)
         quantize(ops["bb"], 0, 128)
+        interleave("vector", ops["w0"], 128, 256)
+        z_chunk(3, 0)
+        z_out("scalar", 1, 3)
+        quantize(ops["z"], 0, 128)
+        interleave("scalar", ops["w0"], 256, 384)
+        interleave("vector", ops["w0"], 384, 512)
+        quantize(ops["z"], 128, 256)
+        z_out("scalar", 3, 0)
+        interleave("vector", ops["w0"], 0, 128)
+        z_chunk(2, 2)
+        interleave("vector", ops["w10"], 0, 128)
         z_out("scalar", 2, 2)
-        quantize(ops["w10"], 0, 256)
-        interleave("vector", ops["w00"], 0, 192)
-        quantize(ops["z"], 384, 512)
-        low_rank(1)
+        quantize(ops["w0"], 0, 256)
         low_rank(0)
-        warm(3, 8)
-        quantize(ops["w00"], 0, 256)
-        low_out("scalar", 1, 0, 2)
-        y_part(2, 0, 0, 2)
-        low_out("scalar", 2, 0, 2)
-        interleave("vector", ops["w01"], 0, 256)
+        low_rank(1)
+        quantize(ops["w10"], 0, 128)
+        interleave("vector", ops["w10"], 128, 256)
+        y_part(1, 0, 0, 2)
+        quantize(ops["z"], 384, 512)
         low_out("scalar", 0, 0, 2)
         quantize(ops["z"], 256, 384)
-        y_part(1, 1, 0, 2)
-        interleave("vector", ops["w13"], 0, 64)
+        quantize(ops["w10"], 128, 256)
+        quantize(ops["w0"], 256, 512)
+        low_out("scalar", 1, 0, 2)
+        interleave("vector", ops["w11"], 0, 128)
         low_rank(3)
         low_rank(2)
-        quantize(ops["w01"], 0, 256)
-        add(2, 0, 0, 2)
-        interleave("scalar", ops["w13"], 64, 128)
-        quantize(ops["w13"], 0, 128)
-        interleave("scalar", ops["w12"], 32, 128)
-        low_out("scalar", 1, 2, 4)
-        y_part(3, 1, 2, 4)
-        interleave("vector", ops["w12"], 0, 32)
-        add(1, 1, 0, 2)
-        y_part(0, 0, 2, 4)
+        interleave("scalar", ops["w11"], 128, 256)
         low_out("scalar", 0, 2, 4)
-        y_part(0, 3, 0, 2)
-        quantize(ops["w12"], 0, 128)
-        y_part(2, 2, 0, 2)
-        low_out("scalar", 2, 2, 4)
-        finish("vector", 0, 0, 2, "sync")
-        low_out("scalar", 3, 0, 2)
-        add(3, 1, 2, 4)
-        finish("vector", 1, 0, 2, "sync")
+        low_out("scalar", 1, 2, 4)
+        y_part(0, 0, 2, 4)
+        quantize(ops["w11"], 128, 256)
+        quantize(ops["w11"], 0, 128)
+        y_part(2, 1, 0, 2)
+        add(1, 0, 0, 2)
+        y_part(3, 1, 2, 4)
+        y_part(3, 3, 0, 2)
         add(0, 0, 2, 4)
+        low_out("scalar", 2, 0, 2)
+        add(2, 1, 0, 2)
+        low_out("scalar", 3, 0, 2)
+        finish("scalar", 0, 0, 2)
+        low_out("scalar", 2, 2, 4)
+        y_part(1, 2, 0, 2)
+        finish("vector", 0, 2, 4)
+        finish("scalar", 1, 0, 2)
+        add(3, 1, 2, 4)
         y_part(1, 2, 2, 4)
         low_out("scalar", 3, 2, 4)
-        add(0, 3, 0, 2)
-        add(2, 2, 0, 2)
+        y_part(2, 3, 2, 4)
+        store(0, 0, 4)
+        add(3, 3, 0, 2)
+        finish("vector", 1, 2, 4)
+        finish("scalar", 3, 0, 2)
         add(1, 2, 2, 4)
-        y_part(3, 3, 2, 4)
-        add(3, 3, 2, 4)
-        finish("scalar", 1, 2, 4, "sync")
-        finish("scalar", 0, 2, 4, "sync")
-        finish("scalar", 3, 0, 2, "sync")
-        finish("scalar", 2, 0, 2, "sync")
-        finish("vector", 2, 2, 4, "sync")
-        finish("vector", 3, 2, 4, "sync")
+        add(1, 2, 0, 2)
+        store(1, 0, 4)
+        finish("scalar", 2, 2, 4)
+        add(2, 3, 2, 4)
+        finish("vector", 2, 0, 2)
+        store(3, 0, 2)
+        finish("scalar", 3, 2, 4)
+        store(2, 0, 4)
+        store(3, 2, 4)

@@ -132,7 +132,7 @@ def tile_rows_lora_relu_bias_kernel(tc, x, w, a, bb, b, out):
         def warm(bank, count):
             for i in range(count):
                 cols = slice(T * (i % 4), T * (i % 4 + 1))
-                mx(whole[bank][:, cols], a_codes1[:, 0:T], a_scales1[:, 0:T], a_codes1[:, T : 2 * T], a_scales1[:, T : 2 * T], True, True)
+                mx(whole[bank][:, cols], a_codes[:, 0, :], a_scales[:, 0, :], a_codes[:, 1, :], a_scales[:, 1, :], True, True)
 
         def window(table, s, i):
             name, c0 = table[s, i]
@@ -192,6 +192,7 @@ def tile_rows_lora_relu_bias_kernel(tc, x, w, a, bb, b, out):
         deal_a("vector", 0)
         quantize_a()
         replicate_a()
+        warm(2, 22)
         interleave("vector", ops["x0"], 0, 128)
         interleave("scalar", ops["x0"], 256, 384)
         interleave("vector", ops["x0"], 128, 256)
@@ -226,7 +227,9 @@ def tile_rows_lora_relu_bias_kernel(tc, x, w, a, bb, b, out):
         z_out("scalar", 2, 2)
         quantize(ops["w0"], 0, 256)
         low_rank(0)
+        warm(3, 4)
         low_rank(1)
+        warm(3, 8)
         quantize(ops["w10"], 0, 128)
         interleave("vector", ops["w10"], 128, 256)
         y_part(1, 0, 0, 2)

from contextlib import ExitStack

import concourse.mybir as mybir

K, R, M, N = 1024, 128, 512, 512
FLOPS = 2 * K * R * N + 2 * K * M * N + 2 * R * M * N

F32 = mybir.dt.float32
BF16 = mybir.dt.bfloat16
U32 = mybir.dt.uint32
I32 = mybir.dt.int32
U8 = mybir.dt.uint8
FP8X4 = mybir.dt.float8_e4m3fn_x4
ACT = mybir.ActivationFunctionType
ALU = mybir.AluOpType

P = 128
PACK = 4
K_PASS = P * PACK
QUAD = 32
T = 128


def tile_rows_lora_relu_bias_kernel(tc, x, w, a, bb, b, out):
    nc = tc.nc
    with ExitStack() as ctx:
        sb = ctx.enter_context(tc.tile_pool(name="sb", bufs=1))
        ps = ctx.enter_context(tc.psum_pool(name="ps", bufs=1))
        ctx.enter_context(tc.manual_schedule())

        whole = [ps.tile([P, 512], F32, name="whole%d" % i) for i in range(4)]
        rowb = [ps.tile([P, 512], F32, name="rowb%d" % i) for i in range(4)]

        def operand(name, width):
            return {
                "raw": sb.tile([P, PACK, width], F32, name=name + "_raw", align_bytes=64),
                "grp": sb.tile([P, width, PACK], BF16, name=name + "_grp", align_bytes=64),
                "codes": sb.tile([P, width], U32, name=name + "_codes", align_bytes=64),
                "scales": sb.tile([P, width], U8, name=name + "_scales", align_bytes=64),
            }

        def load(op, src, s, c0, width):
            rows = src[s * K_PASS : (s + 1) * K_PASS, c0 : c0 + width]
            nc.sync.dma_start(out=op["raw"][:], in_=rows.rearrange("(p j) c -> p j c", j=PACK))

        def interleave(engine, op, c0, c1):
            dst = op["grp"][:, c0:c1, :].rearrange("p (c i) j -> p c j i", i=4)
            src = op["raw"][:, :, c0:c1].rearrange("p j (c i) -> p c j i", i=4)
            if engine == "vector":
                nc.vector.tensor_copy(out=dst, in_=src)
            else:
                nc.scalar.copy(out=dst, in_=src)

        def quantize(op, c0, c1):
            nc.vector.quantize_mx(
                out=op["codes"][:, c0:c1].bitcast(FP8X4),
                scales=op["scales"][:, c0:c1],
                in_=op["grp"][:, c0:c1, :].rearrange("p c j -> p (c j)"),
            )

        def mx(dst, lc, ls, rc, rs, start, stop):
            nc.tensor.matmul_mx(
                out=dst, lhsT=lc.bitcast(FP8X4), lhsT_scale=ls, rhs=rc.bitcast(FP8X4), rhs_scale=rs,
                start=start, stop=stop,
            )

        a_raw = sb.tile([P, 2, PACK, R], F32, align_bytes=64)
        a_grp = sb.tile([P, 2, R * PACK], BF16, align_bytes=64)
        a_codes1 = sb.tile([P, 2 * R], U32, align_bytes=64)
        a_scales1 = sb.tile([P, 2 * R], U8, align_bytes=64)
        a_codes = sb.tile([P, 8, T], U32, align_bytes=64)
        a_scales = sb.tile([P, 8, T], U8, align_bytes=64)
        ops = {"bb": operand("bb", T)}
        ops["x0"] = operand("x0", 512)
        ops["x1"] = operand("x1", 512)
        ops["w0"] = operand("w0", 512)
        ops["w10"] = operand("w10", 256)
        ops["w11"] = operand("w11", 256)
        xm = {(0, 0): ("x0", 0), (0, 1): ("x0", 128), (0, 2): ("x0", 256), (0, 3): ("x0", 384), (1, 0): ("x1", 0), (1, 1): ("x1", 128), (1, 2): ("x1", 256), (1, 3): ("x1", 384)}
        wm = {(0, 0): ("w0", 0), (0, 1): ("w0", 128), (0, 2): ("w0", 256), (0, 3): ("w0", 384), (1, 0): ("w10", 0), (1, 1): ("w10", 128), (1, 2): ("w11", 0), (1, 3): ("w11", 128)}
        bo = ops["bb"]
        z_grp = sb.tile([P, N, PACK], BF16, align_bytes=64)
        z_codes = sb.tile([P, N], U32, align_bytes=64)
        z_scales = sb.tile([P, N], U8, align_bytes=64)
        ops["z"] = {"grp": z_grp, "codes": z_codes, "scales": z_scales}
        bias_rows = sb.tile([P, QUAD], F32, align_bytes=64)
        bias = sb.tile([P, QUAD], F32, align_bytes=64)
        low = [sb.tile([P, N], F32, name="low%d" % g) for g in range(4)]
        tot = [sb.tile([P, N], F32, name="tot%d" % g) for g in range(4)]
        res = [sb.tile([P, N], F32, name="res%d" % g) for g in range(4)]

        nc.vector.memset(bias_rows[:], 0.0)
        b_rows = b.rearrange("(g q i) o -> q g (i o)", g=4, q=4)
        for q in range(4):
            nc.scalar.dma_start(out=bias_rows[QUAD * q : QUAD * q + 4, :], in_=b_rows[q])
        nc.sync.dma_start(out=a_raw[:].rearrange("p s j r -> p s (j r)"), in_=a.rearrange("(s p j) r -> p s (j r)", s=2, j=PACK))
        load(ops["x0"], x, 0, 0, 512)
        load(ops["x1"], x, 1, 0, 512)
        for g in (0, 2, 1, 3):
            nc.sync.dma_start(out=bo["raw"][QUAD * g : QUAD * (g + 1), :, :], in_=bb[:, T * g : T * (g + 1)].rearrange("(p j) c -> p j c", j=PACK))
        load(ops["w0"], w, 0, 0, 512)
        load(ops["w10"], w, 1, 0, 256)
        load(ops["w11"], w, 1, 256, 256)

        nc.vector.memset(a_scales1[:].bitcast(U32), 0)

        def deal_a(engine, s):
            if engine == "vector":
                dst = a_grp[:, s, :].rearrange("p (t m j) -> p t m j", t=4, j=PACK)
                src = a_raw[:, s, :, :].rearrange("p j (m t) -> p t m j", t=4)
                nc.vector.tensor_copy(out=dst, in_=src)
            else:
                dst = a_grp[:, s, :].rearrange("p (t m j) -> p m t j", t=4, j=PACK)
                src = a_raw[:, s, :, :].rearrange("p j (m t) -> p m t j", t=4)
                nc.scalar.activation(out=dst, in_=src, func=ACT.Copy)

        def quantize_a():
            nc.vector.quantize_mx(
                out=a_codes1[:].bitcast(FP8X4), scales=a_scales1[:], in_=a_grp[:].rearrange("p s c -> p (s c)")
            )

        def replicate_a():
            nc.vector.tensor_copy(
                out=a_codes[:].bitcast(I32).rearrange("p u (g m) -> p u g m", g=4),
                in_=a_codes1[:].bitcast(I32).rearrange("p (u m) -> p u m", m=QUAD).unsqueeze(2).to_broadcast([P, 8, 4, QUAD]),
            )
            nc.vector.tensor_copy(
                out=a_scales[:].bitcast(I32).rearrange("p u (g m) -> p u g m", g=4),
                in_=a_scales1[:].bitcast(I32).rearrange("p (u m) -> p u m", m=8).unsqueeze(2).to_broadcast([P, 8, 4, 8]),
            )

        def warm(bank, count):
            for i in range(count):
                cols = slice(T * (i % 4), T * (i % 4 + 1))
                mx(whole[bank][:, cols], a_codes[:, 0, :], a_scales[:, 0, :], a_codes[:, 1, :], a_scales[:, 1, :], True, True)

        def window(table, s, i):
            name, c0 = table[s, i]
            return ops[name]["codes"][:, c0 : c0 + T], ops[name]["scales"][:, c0 : c0 + T]

        def z_chunk(c, bank):
            for t in range(4):
                for s in range(2):
                    xc, xs = window(xm, s, c)
                    mx(whole[bank][:, T * t : T * (t + 1)], a_codes[:, 4 * s + t, :], a_scales[:, 4 * s + t, :],
                       xc, xs, s == 0, s == 1)

        def copy(engine, dst, src):
            if engine == "vector":
                nc.vector.tensor_copy(out=dst, in_=src)
            else:
                nc.scalar.copy(out=dst, in_=src)

        def z_out(engine, c, bank):
            copy(engine, z_grp[:, T * c : T * (c + 1), :], whole[bank][:].rearrange("p (t n) -> p n t", t=4))

        def low_rank(c):
            cols = slice(T * c, T * (c + 1))
            for g in range(4):
                rows = slice(QUAD * g, QUAD * (g + 1))
                mx(rowb[g][:, cols], bo["codes"][rows, :], bo["scales"][rows, :],
                   z_codes[rows, cols], z_scales[rows, cols], True, True)

        def low_out(engine, g, c0, c1):
            copy(engine, low[g][:, T * c0 : T * c1], rowb[g][:, T * c0 : T * c1])

        def y_part(bank, g, c0, c1):
            for c in range(c0, c1):
                for s in range(2):
                    wc, ws = window(wm, s, g)
                    xc, xs = window(xm, s, c)
                    mx(whole[bank][:, T * c : T * (c + 1)], wc, ws, xc, xs, s == 0, s == 1)

        def add(bank, g, c0, c1):
            cols = slice(T * c0, T * c1)
            nc.vector.tensor_tensor(out=tot[g][:, cols], in0=whole[bank][:, cols], in1=low[g][:, cols], op=ALU.add)

        def finish(engine, g, c0, c1):
            cols = slice(T * c0, T * c1)
            if engine == "vector":
                nc.vector.tensor_scalar(out=res[g][:, cols], in0=tot[g][:, cols], scalar1=bias[:, g : g + 1], scalar2=0.0, op0=ALU.add, op1=ALU.max)
            elif engine == "gpsimd":
                nc.gpsimd.tensor_scalar(out=res[g][:, cols], in0=tot[g][:, cols], scalar1=bias[:, g : g + 1], scalar2=0.0, op0=ALU.add, op1=ALU.max)
            else:
                nc.scalar.activation(out=res[g][:, cols], in_=tot[g][:, cols], func=ACT.Relu, bias=bias[:, g : g + 1])

        def store(g, c0, c1):
            cols = slice(T * c0, T * c1)
            nc.sync.dma_start(out=out[T * g : T * (g + 1), cols], in_=res[g][:, cols])

        deal_a("scalar", 1)
        deal_a("vector", 0)
        quantize_a()
        replicate_a()
        warm(2, 22)
        interleave("vector", ops["x0"], 0, 128)
        interleave("scalar", ops["x0"], 256, 384)
        interleave("vector", ops["x0"], 128, 256)
        quantize(ops["x0"], 0, 256)
        interleave("vector", ops["x0"], 384, 512)
        nc.vector.transpose(out=bias[:], in_=bias_rows[:])
        interleave("vector", ops["x1"], 0, 128)
        quantize(ops["x1"], 0, 128)
        interleave("scalar", ops["x1"], 128, 256)
        quantize(ops["x1"], 128, 256)
        quantize(ops["x0"], 256, 512)
        z_chunk(0, 1)
        interleave("vector", ops["x1"], 256, 384)
        z_chunk(1, 3)
        interleave("scalar", ops["x1"], 384, 512)
        z_out("scalar", 0, 1)
        interleave("vector", ops["bb"], 0, 128)
        quantize(ops["x1"], 384, 512)
        quantize(ops["x1"], 256, 384)
        quantize(ops["bb"], 0, 128)
        interleave("vector", ops["w0"], 128, 256)
        z_chunk(3, 0)
        z_out("scalar", 1, 3)
        quantize(ops["z"], 0, 128)
        interleave("scalar", ops["w0"], 256, 384)
        interleave("vector", ops["w0"], 384, 512)
        quantize(ops["z"], 128, 256)
        z_out("scalar", 3, 0)
        interleave("vector", ops["w0"], 0, 128)
        z_chunk(2, 2)
        interleave("vector", ops["w10"], 0, 128)
        z_out("scalar", 2, 2)
        quantize(ops["w0"], 0, 256)
        low_rank(0)
        warm(3, 4)
        low_rank(1)
        warm(3, 8)
        quantize(ops["w10"], 0, 128)
        interleave("vector", ops["w10"], 128, 256)
        y_part(1, 0, 0, 2)
        quantize(ops["z"], 384, 512)
        low_out("scalar", 0, 0, 2)
        quantize(ops["z"], 256, 384)
        quantize(ops["w10"], 128, 256)
        quantize(ops["w0"], 256, 512)
        low_out("scalar", 1, 0, 2)
        interleave("vector", ops["w11"], 0, 128)
        low_rank(3)
        low_rank(2)
        interleave("scalar", ops["w11"], 128, 256)
        low_out("scalar", 0, 2, 4)
        low_out("scalar", 1, 2, 4)
        y_part(0, 0, 2, 4)
        quantize(ops["w11"], 128, 256)
        quantize(ops["w11"], 0, 128)
        y_part(2, 1, 0, 2)
        add(1, 0, 0, 2)
        y_part(3, 1, 2, 4)
        y_part(3, 3, 0, 2)
        add(0, 0, 2, 4)
        low_out("scalar", 2, 0, 2)
        add(2, 1, 0, 2)
        low_out("scalar", 3, 0, 2)
        finish("scalar", 0, 0, 2)
        low_out("scalar", 2, 2, 4)
        y_part(1, 2, 0, 2)
        finish("vector", 0, 2, 4)
        finish("scalar", 1, 0, 2)
        add(3, 1, 2, 4)
        y_part(1, 2, 2, 4)
        low_out("scalar", 3, 2, 4)
        y_part(2, 3, 2, 4)
        store(0, 0, 4)
        add(3, 3, 0, 2)
        finish("vector", 1, 2, 4)
        finish("scalar", 3, 0, 2)
        add(1, 2, 2, 4)
        add(1, 2, 0, 2)
        store(1, 0, 4)
        finish("scalar", 2, 2, 4)
        add(2, 3, 2, 4)
        finish("vector", 2, 0, 2)
        store(3, 0, 2)
        finish("scalar", 3, 2, 4)
        store(2, 0, 4)
        store(3, 2, 4)
